import numpy as np
import ml_dtypes


def mxq(x, axis, fmt="e4m3"):
    dtype, down = {"e4m3": (ml_dtypes.float8_e4m3fn, 7), "e5m2": (ml_dtypes.float8_e5m2, 14)}[fmt]
    v = np.moveaxis(np.asarray(x, np.float32).astype(ml_dtypes.bfloat16).astype(np.float64), axis, -1)
    blocks = v.reshape(v.shape[:-1] + (-1, 32))
    amax = np.abs(blocks).max(-1, keepdims=True)
    byte = np.maximum(np.where(amax > 0, np.frexp(amax)[1] - 1 + 127, 0) - down, 1)
    scale = np.exp2(byte - 127.0)
    codes = (blocks / scale).astype(np.float32).astype(dtype).astype(np.float64)
    return np.moveaxis((codes * scale).reshape(v.shape), -1, axis)


WIDE = False


def mx_kscale(k):
    if not WIDE:
        return np.ones(k)
    levels = np.array([10, -10, 5, -5, 0])
    if k % 512:
        return np.exp2(np.random.permutation(np.resize(levels, k // 32))).repeat(32)
    a = np.empty((k // 512, 16))
    for p in range(k // 512):
        a[p, :8] = np.random.permutation(np.resize(levels, 8))
        for g in range(8):
            far = levels[np.abs(levels - a[p, g]) >= 10]
            a[p, g + 8] = far[np.random.randint(len(far))]
    return np.exp2(a.ravel()).repeat(32)


BF16 = ml_dtypes.bfloat16


def bf(x):
    return np.asarray(x, np.float32).astype(BF16)


def f64(x):
    return np.asarray(x).astype(np.float64)


E2M1 = np.array([0.0, 0.5, 1.0, 1.5, 2.0, 3.0, 4.0, 6.0, -0.0, -0.5, -1.0, -1.5, -2.0, -3.0, -4.0, -6.0])


def pack_weight(w, fmt):
    k, n = w.shape
    w = f64(bf(w)).reshape(k // 32, 32, n)
    amax = np.abs(w).max(1)
    if fmt == "e4m3":
        byte = np.frexp(amax)[1] - 1 + 127 - 7
    else:
        mant, ex = np.frexp(amax / 6.0)
        byte = np.where(mant > 0.5, ex, ex - 1) + 127
    byte = np.clip(np.where(amax > 0, byte, 1), 1, 254)
    scaled = (w * np.exp2(127.0 - byte)[:, None, :]).reshape(k, n).astype(np.float32)
    by_word = np.ascontiguousarray(scaled.reshape(k // 512, 128, 4, n).transpose(0, 1, 3, 2))
    if fmt == "e4m3":
        words = by_word.astype(ml_dtypes.float8_e4m3fn).view(np.uint8)
    else:
        c = by_word.astype(ml_dtypes.float4_e2m1fn).view(np.uint8) & 0xF
        words = c[..., 0::2] | (c[..., 1::2] << 4)
    return np.ascontiguousarray(words), np.ascontiguousarray(byte.astype(np.uint8).reshape(k // 512, 16, n))


def unpack_weight(words, scales, fmt):
    g, p, n, _ = words.shape
    if fmt == "e4m3":
        vals = np.ascontiguousarray(words).view(ml_dtypes.float8_e4m3fn).astype(np.float64)
    else:
        nib = np.empty((g, p, n, 4), np.uint8)
        nib[..., 0::2] = words & 0xF
        nib[..., 1::2] = words >> 4
        vals = E2M1[nib]
    vals = vals * np.repeat(np.exp2(scales.astype(np.float64) - 127.0), 8, axis=1)[..., None]
    return vals.transpose(0, 1, 3, 2).reshape(g * 512, n)
def pack4(w):
    words, scales = pack_weight(w, "e2m1")
    return words.reshape(words.shape[0], 128, -1), scales


def unpack4(words, scales):
    return unpack_weight(words.reshape(words.shape[0], 128, -1, 2), scales, "e2m1")


N, D, H, O = 1024, 1024, 1024, 512

BETA = 0.5


def nudged_states(a, f, beta):
    hp = np.tanh(a + beta * f)
    hm = np.tanh(a - beta * f)
    return hp, hm


def draw0():
    s, u, t = mx_kscale(D), mx_kscale(O), mx_kscale(N)
    x = bf(np.random.standard_normal((N, D)))
    p = bf((1.0 + 0.1 * np.random.standard_normal(D)) * s)
    w1_words, w1_scales = pack4(np.random.standard_normal((D, H)) / np.sqrt(D) / s[:, None])
    e = bf(np.random.standard_normal((N, O)) * u[None, :])
    w2_words, w2_scales = pack4((np.random.standard_normal((H, O)) / np.sqrt(O) / u[None, :]).T)
    return {"x": x,
            "p": p,
            "w1_words": w1_words,
            "w1_scales": w1_scales,
            "e": e,
            "w2_words": w2_words,
            "w2_scales": w2_scales,
            "r": bf((1.0 + 0.1 * np.random.standard_normal(N)) * t),
            "g": bf((1.0 + 0.1 * np.random.standard_normal(N)) / t)}


def core(x, p, w1_words, w1_scales, e, w2_words, w2_scales, r, g):
    x, p, e, r, g = f64(x), f64(p), f64(e), f64(r), f64(g)
    n = x.shape[0]
    a = mxq(x * p[None, :], 1, "e4m3") @ unpack4(w1_words, w1_scales)
    f = mxq(e, 1, "e4m3") @ unpack4(w2_words, w2_scales)
    hp, hm = nudged_states(a, f, BETA)
    d = (hp - hm) * g[:, None] / (2.0 * BETA * np.sqrt(n))
    xr = x * r[:, None]
    return mxq(xr, 0, "e4m3").T @ mxq(d, 0, "e4m3")


def e4m3fn_bytes(y):
    return np.clip(np.asarray(y, np.float64), -448.0, 448.0).astype(np.float32).astype(ml_dtypes.float8_e4m3fn).view(np.uint8)


def e4m3fn_values(b):
    return np.asarray(b, np.uint8).view(ml_dtypes.float8_e4m3fn).astype(np.float64)


def setup_inputs():
    d = draw0()
    x0 = np.asarray(d['e']).astype(np.float64)
    s = (np.max(np.abs(x0), axis=(0,), keepdims=True) / 448.0).astype(np.float32)
    out = {}
    for k, v in d.items():
        if k == 'e':
            out['e_bytes'] = e4m3fn_bytes(x0 / s.astype(np.float64))
            out['e_scale'] = s
        else:
            out[k] = v
    return out


def reference(x, p, w1_words, w1_scales, e_bytes, e_scale, w2_words, w2_scales, r, g):
    return core(x, p, w1_words, w1_scales, e4m3fn_values(e_bytes) * e_scale.astype(np.float64), w2_words, w2_scales, r, g)

@@ -1,0 +1,677 @@
+from contextlib import ExitStack
+
+import concourse.mybir as mybir
+from concourse.masks import make_identity
+
+F32 = mybir.dt.float32
+BF16 = mybir.dt.bfloat16
+U32 = mybir.dt.uint32
+I32 = mybir.dt.int32
+U8 = mybir.dt.uint8
+E4M3 = mybir.dt.float8_e4m3fn
+FP8X4 = mybir.dt.float8_e4m3fn_x4
+FP4X4 = mybir.dt.float4_e2m1fn_x4
+MULT = mybir.AluOpType.mult
+SUB = mybir.AluOpType.subtract
+TANH = mybir.ActivationFunctionType.Tanh
+COPY = mybir.ActivationFunctionType.Copy
+
+P = 128
+N, D, H, O = 1024, 1024, 1024, 512
+FLOPS = 2 * N * D * H + 2 * N * O * H + 2 * N * D * H
+G = 2
+T = 4
+W = 512
+CHUNKS = ((0, 512), (512, 256), (768, 256))
+
+
+def tile_centredequilibriumpropupdate_w4_kernel(
+    tc, x, p, w1_words, w1_scales, e_bytes, e_scale, w2_words, w2_scales, r, g, out
+):
+    nc = tc.nc
+    with ExitStack() as ctx:
+        keep = ctx.enter_context(tc.tile_pool(name="keep", bufs=1))
+        work = ctx.enter_context(tc.tile_pool(name="work", bufs=3))
+        psum = ctx.enter_context(tc.psum_pool(name="psum", bufs=4))
+        ctx.enter_context(tc.manual_schedule())
+
+        xt = [keep.tile([P, T, D], BF16, name="xt%d" % i, align_bytes=64) for i in range(G)]
+        eb = keep.tile([P, G, T, O], U8, name="eb", align_bytes=64)
+        pb = keep.tile([P, D], BF16, name="pb", align_bytes=64)
+        pbp = keep.tile([P, D], BF16, name="pbp", align_bytes=64)
+        es_raw = keep.tile([P, O], F32, name="es_raw", align_bytes=64)
+        es_half = keep.tile([P, O], F32, name="es_half", align_bytes=64)
+        w1t = keep.tile([P, 2, 2 * H], U8, name="w1t", align_bytes=64)
+        w2t = keep.tile([P, 2 * H], U8, name="w2t", align_bytes=64)
+        wsc = keep.tile([P, 3, H], U8, name="wsc", align_bytes=64)
+        rb = keep.tile([P, G, T], BF16, name="rb", align_bytes=64)
+        gb = keep.tile([P, G, T], BF16, name="gb", align_bytes=64)
+        rf = keep.tile([P, G, T], F32, name="rf", align_bytes=64)
+        gs = keep.tile([P, G, T], F32, name="gs", align_bytes=64)
+        ident = keep.tile([P, P], F32, name="ident", align_bytes=64)
+        warm = keep.tile([P, 2], F32, name="warm", align_bytes=64)
+        xc = keep.tile([P, 8, 2, P], U32, name="xc", align_bytes=64)
+        xs = keep.tile([P, 8, 2, P], U8, name="xs", align_bytes=64)
+        ec = keep.tile([P, 8, 2, P], U32, name="ec", align_bytes=64)
+        es = keep.tile([P, 8, 2, P], U8, name="es", align_bytes=64)
+        rc = keep.tile([P, G, D], U32, name="rc", align_bytes=64)
+        rs = keep.tile([P, G, D], U8, name="rs", align_bytes=64)
+        dc = [keep.tile([P, G, w], U32, name="dc%d" % c, align_bytes=64) for c, (lo, w) in enumerate(CHUNKS)]
+        dsc = [keep.tile([P, G, w], U8, name="dsc%d" % c, align_bytes=64) for c, (lo, w) in enumerate(CHUNKS)]
+        hpm = {
+            (i, c, s): keep.tile([P, T, W], F32, name="h%d%d%d" % (i, c, s), align_bytes=64)
+            for i in range(G)
+            for c in range(2)
+            for s in range(2)
+        }
+
+        xv = x.rearrange("(g p t) d -> g p t d", g=G, p=P, t=T)
+        ev = e_bytes.rearrange("(g p t) o -> g p t o", g=G, p=P, t=T)
+        w1v = w1_words.rearrange("g p w -> p g w")
+
+        def load_w(lo, hi):
+            nc.sync.dma_start(out=w1t[:, :, 2 * lo : 2 * hi], in_=w1v[:, :, 2 * lo : 2 * hi])
+            nc.sync.dma_start(out=w2t[:, 2 * lo : 2 * hi], in_=w2_words[0, :, 2 * lo : 2 * hi])
+
+
+        ident_bf = keep.tile([P, P], BF16, name="ident_bf", align_bytes=64)
+        nc.gpsimd.memset(wsc[:].rearrange("p k n -> p (k n)").bitcast(I32), 0)
+        make_identity(nc, ident[:])
+        make_identity(nc, ident_bf[:])
+        nc.vector.memset(warm[:], 0.0)
+        nc.scalar.activation(out=warm[:, 1:2], in_=warm[:, 0:1], func=TANH)
+
+        def load_x(i, t0, t1):
+            nc.sync.dma_start(out=xt[i][:, t0:t1, :], in_=xv[i, :, t0:t1, :])
+
+        def load_pb():
+            nc.sync.dma_start(out=pb[:], in_=p.partition_broadcast(P))
+
+        def load_es():
+            nc.sync.dma_start(out=es_raw[:], in_=e_scale.rearrange("o k -> (o k)").partition_broadcast(P))
+
+        def load_e(i):
+            nc.sync.dma_start(out=eb[:, i, :, :], in_=ev[i])
+
+        def load_rg():
+            nc.sync.dma_start(out=rb[:], in_=r.rearrange("(g p t) -> p g t", g=G, p=P, t=T))
+            nc.sync.dma_start(out=gb[:], in_=g.rearrange("(g p t) -> p g t", g=G, p=P, t=T))
+
+        def load_scales1():
+            for q in range(4):
+                nc.sync.dma_start(
+                    out=wsc[32 * q : 32 * q + 4, 0:2, :].bitcast(I32),
+                    in_=w1_scales[:, 4 * q : 4 * q + 4, :].rearrange("g q n -> q g n").bitcast(I32),
+                )
+        def load_scales2():
+            for q in range(4):
+                nc.sync.dma_start(
+                    out=wsc[32 * q : 32 * q + 4, 2, :].bitcast(I32), in_=w2_scales[0, 4 * q : 4 * q + 4, :].bitcast(I32)
+                )
+
+        xpw = {}
+        eww = {}
+        xg = {}
+        eg = {}
+        xb = {}
+        ebk = {}
+
+        def es_prep():
+            nc.scalar.activation(out=es_half[:], in_=es_raw[:], func=COPY, scale=0.5)
+
+        def gs_prep():
+            nc.scalar.activation(
+                out=gs[:].rearrange("p g t -> p (g t)"),
+                in_=gb[:].rearrange("p g t -> p (g t)"),
+                func=COPY,
+                scale=1.0 / 32.0,
+            )
+
+        def pb_prep():
+            nc.vector.tensor_copy(
+                out=pbp[:].rearrange("p (u q e) -> p u q e", u=2, e=2),
+                in_=pb[:].rearrange("p (q u e) -> p u q e", u=2, e=2),
+            )
+
+        def x_mul(b):
+            xp = work.tile([P, D], BF16, name="xp", align_bytes=64)
+            nc.vector.tensor_tensor(
+                out=xp[:].rearrange("p (u q e) -> p u q e", u=2, e=2),
+                in0=xt[b // T][:, b % T, :].rearrange("p (q u e) -> p u q e", u=2, e=2),
+                in1=pbp[:].rearrange("p (u q e) -> p u q e", u=2, e=2),
+                op=MULT,
+            )
+            xpw[b] = xp
+
+        def e_mul(b):
+            ew = work.tile([P, O], BF16, name="ew", align_bytes=64)
+            nc.vector.tensor_tensor(out=ew[:], in0=eb[:, b // T, b % T, :].bitcast(E4M3), in1=es_half[:], op=MULT)
+            eww[b] = ew
+
+        def x_turn(b):
+            xb[b] = psum.tile([P, 2, 2, P], F32, name="m")
+            words = xpw[b][:].bitcast(F32)
+            for k in range(2):
+                for u in range(2):
+                    nc.tensor.transpose(xb[b][:, k, u, :], words[:, 256 * u + 128 * k : 256 * u + 128 * (k + 1)], ident[:])
+
+        def x_copy(b):
+            if b % 2 == 0:
+                xg[b // 2] = work.tile([P, 2, 2, P, 4], BF16, name="xg", bufs=2, align_bytes=64)
+            grouped = xg[b // 2][:, b % 2].rearrange("p k n j -> p k (n j)").bitcast(F32)
+            nc.scalar.copy(
+                out=grouped.rearrange("p k (n u) -> p k n u", u=2), in_=xb[b][:].rearrange("p k u n -> p k n u")
+            )
+
+        def e_turn(b, n):
+            ebk[b] = psum.tile([P, n, 2, P], F32, name="m")
+            for j in range(n):
+                words = eww[b + j][:].bitcast(F32)
+                for u in range(2):
+                    nc.tensor.transpose(ebk[b][:, j, u, :], words[:, u:256:2], ident[:])
+
+        def e_copy(b, n):
+            if b % 2 == 0:
+                eg[b // 2] = work.tile([P, 2, 2, P, 4], BF16, name="eg", bufs=2, align_bytes=64)
+            h = b % 2
+            grouped = eg[b // 2][:, h : h + n, 0].rearrange("p b n j -> p b (n j)").bitcast(F32)
+            nc.scalar.copy(
+                out=grouped.rearrange("p b (n u) -> p b n u", u=2), in_=ebk[b][:].rearrange("p b u n -> p b n u")
+            )
+
+        def x_quant(q):
+            nc.vector.quantize_mx(
+                out=xc[:, 2 * q : 2 * q + 2].rearrange("p b k n -> p (b k n)").bitcast(FP8X4),
+                scales=xs[:, 2 * q : 2 * q + 2].rearrange("p b k n -> p (b k n)"),
+                in_=xg[q][:].rearrange("p b k n j -> p (b k n j)"),
+            )
+
+        def x_quant1(b):
+            nc.vector.quantize_mx(
+                out=xc[:, b].rearrange("p k n -> p (k n)").bitcast(FP8X4),
+                scales=xs[:, b].rearrange("p k n -> p (k n)"),
+                in_=xg[b // 2][:, b % 2].rearrange("p k n j -> p (k n j)"),
+            )
+
+        def e_neg(b, n):
+            h = b % 2
+            flat = eg[b // 2][:, h : h + n].rearrange("p b s n j -> p b s (n j)")
+            nc.vector.tensor_scalar(out=flat[:, :, 1], in0=flat[:, :, 0], scalar1=-1.0, scalar2=None, op0=MULT)
+
+        def e_quant(b, n):
+            h = b % 2
+            nc.vector.quantize_mx(
+                out=ec[:, b : b + n].rearrange("p b s n -> p (b s n)").bitcast(FP8X4),
+                scales=es[:, b : b + n].rearrange("p b s n -> p (b s n)"),
+                in_=eg[b // 2][:, h : h + n].rearrange("p b s n j -> p (b s n j)"),
+            )
+
+        ub = {}
+
+        def s1(b, c, s):
+            lo, hi = c * W, (c + 1) * W
+            ub[b, c, s] = psum.tile([P, W], F32, name="u")
+            for k in range(2):
+                nc.tensor.matmul_mx(
+                    out=ub[b, c, s][:],
+                    lhsT=xc[:, b, k, :].bitcast(FP8X4),
+                    lhsT_scale=xs[:, b, k, :],
+                    rhs=w1t[:, k, 2 * lo : 2 * hi].bitcast(FP4X4),
+                    rhs_scale=wsc[:, k, lo:hi],
+                    start=(k == 0),
+                    stop=False,
+                )
+            nc.tensor.matmul_mx(
+                out=ub[b, c, s][:],
+                lhsT=ec[:, b, s, :].bitcast(FP8X4),
+                lhsT_scale=es[:, b, s, :],
+                rhs=w2t[:, 2 * lo : 2 * hi].bitcast(FP4X4),
+                rhs_scale=wsc[:, 2, lo:hi],
+                start=False,
+                stop=True,
+            )
+
+        def tanh(b, c, s):
+            nc.scalar.activation(out=hpm[b // T, c, s][:, b % T, :], in_=ub[b, c, s][:], func=TANH)
+
+        db = {}
+        dg = {}
+
+        def diff(i, c, t0, t1):
+            nc.vector.tensor_tensor(
+                out=hpm[i, c, 0][:, t0:t1, :], in0=hpm[i, c, 0][:, t0:t1, :], in1=hpm[i, c, 1][:, t0:t1, :], op=SUB
+            )
+
+        def new_db(i, c):
+            if (i, c) not in db:
+                db[i, c] = work.tile([P, T, W], BF16, name="db", bufs=3, align_bytes=64)
+
+        def scale_s(i, c, t):
+            new_db(i, c)
+            nc.scalar.activation(out=db[i, c][:, t, :], in_=hpm[i, c, 0][:, t, :], func=COPY, scale=gs[:, i, t : t + 1])
+
+        def scale_v(i, c, t):
+            new_db(i, c)
+            nc.vector.tensor_scalar(
+                out=db[i, c][:, t, :], in0=hpm[i, c, 0][:, t, :], scalar1=gs[:, i, t : t + 1], scalar2=None, op0=MULT
+            )
+
+        def weave_d(i, c, lo, hi):
+            if lo == 0:
+                dg[i, c] = work.tile([P, W, T], BF16, name="dg", bufs=3, align_bytes=64)
+            nc.vector.tensor_copy(
+                out=dg[i, c][:, lo:hi, :].rearrange("p (n j) t -> p n t j", j=4),
+                in_=db[i, c][:, :, lo:hi].rearrange("p t (n j) -> p n t j", j=4),
+            )
+
+        def quant_d(i, c):
+            lo, w = CHUNKS[c]
+            nc.vector.quantize_mx(
+                out=dc[c][:, i, :].bitcast(FP8X4),
+                scales=dsc[c][:, i, :],
+                in_=dg[i, lo // W][:, lo % W : lo % W + w, :].rearrange("p n t -> p (n t)"),
+            )
+
+        xm = {}
+        xw = {}
+        rdiag = {}
+        rbk = {}
+
+        def new_xw(i):
+            if i not in xw:
+                xw[i] = work.tile([P, D, T], BF16, name="xw", bufs=2, align_bytes=64)
+
+        def r_mul(i, t):
+            if i not in xm:
+                xm[i] = work.tile([P, T, D], BF16, name="xm", bufs=1, align_bytes=64)
+            nc.vector.tensor_scalar(
+                out=xm[i][:, t, :], in0=xt[i][:, t, :], scalar1=rb[:, i, t : t + 1], scalar2=None, op0=MULT
+            )
+
+        def r_prep():
+            nc.scalar.activation(
+                out=rf[:].rearrange("p g t -> p (g t)"), in_=rb[:].rearrange("p g t -> p (g t)"), func=COPY
+            )
+
+        def r_mul_s(i, t):
+            if i not in xm:
+                xm[i] = work.tile([P, T, D], BF16, name="xm", bufs=1, align_bytes=64)
+            nc.scalar.activation(out=xm[i][:, t, :], in_=xt[i][:, t, :], func=COPY, scale=rf[:, i, t : t + 1])
+
+        def r_weave(i, q):
+            new_xw(i)
+            w = D // 4
+            nc.vector.tensor_copy(
+                out=xw[i][:, q * w : (q + 1) * w, :].rearrange("p (n j) t -> p n t j", j=4),
+                in_=xm[i][:, :, q * w : (q + 1) * w].rearrange("p t (n j) -> p n t j", j=4),
+            )
+
+        def r_diag(i):
+            rdiag[i] = work.tile([P, T, P], BF16, name="rdiag", bufs=2, align_bytes=64)
+            for t in range(T):
+                nc.vector.tensor_scalar(
+                    out=rdiag[i][:, t, :], in0=ident_bf[:], scalar1=rb[:, i, t : t + 1], scalar2=None, op0=MULT
+                )
+
+        def r_pe(i, q):
+            w = D // 4
+            rbk[i, q] = psum.tile([P, T, w], BF16, name="m")
+            for t in range(T):
+                nc.tensor.matmul(
+                    rbk[i, q][:, t, :],
+                    lhsT=rdiag[i][:, t, :],
+                    rhs=xt[i][:, t, q * w : (q + 1) * w],
+                    start=True,
+                    stop=True,
+                )
+
+        def r_copy(i, q):
+            new_xw(i)
+            w = D // 4
+            nc.scalar.copy(
+                out=xw[i][:, q * w : (q + 1) * w, :], in_=rbk[i, q][:].rearrange("p t n -> p n t")
+            )
+
+        def r_quant(i, lo, hi):
+            nc.vector.quantize_mx(
+                out=rc[:, i, lo:hi].bitcast(FP8X4), scales=rs[:, i, lo:hi], in_=xw[i][:, lo:hi, :].rearrange("p n t -> p (n t)")
+            )
+
+        ob = {}
+        rest = {}
+
+        def s2_last(c, f, i, tag):
+            lo, w = CHUNKS[c]
+            if i == 0:
+                ob[c, f] = psum.tile([P, w], F32, name=tag)
+            nc.tensor.matmul_mx(
+                out=ob[c, f][:],
+                lhsT=rc[:, i, f * P : (f + 1) * P].bitcast(FP8X4),
+                lhsT_scale=rs[:, i, f * P : (f + 1) * P],
+                rhs=dc[c][:, i, :].bitcast(FP8X4),
+                rhs_scale=dsc[c][:, i, :],
+                start=(i == 0),
+                stop=(i == G - 1),
+            )
+
+        def copy_last(c, f, eng):
+            lo, w = CHUNKS[c]
+            if f % 2 == 0:
+                rest[c, f] = work.tile([P, 2, w], F32, name="resl", bufs=4, align_bytes=64)
+            dst = rest[c, f - f % 2][:, f % 2, :]
+            if eng == "V":
+                nc.vector.tensor_copy(out=dst, in_=ob[c, f][:])
+            else:
+                nc.scalar.copy(out=dst, in_=ob[c, f][:])
+
+        def s2(c, f, i, tag):
+            lo, w = CHUNKS[c]
+            nt = 512 // w
+            if i == 0 and f % nt == 0:
+                ob[c, f] = psum.tile([P, nt, w], F32, name=tag)
+            nc.tensor.matmul_mx(
+                out=ob[c, f - f % nt][:, f % nt, :],
+                lhsT=rc[:, i, f * P : (f + 1) * P].bitcast(FP8X4),
+                lhsT_scale=rs[:, i, f * P : (f + 1) * P],
+                rhs=dc[c][:, i, :].bitcast(FP8X4),
+                rhs_scale=dsc[c][:, i, :],
+                start=(i == 0),
+                stop=(i == G - 1),
+            )
+
+        def out_copy(c, f, eng):
+            lo, w = CHUNKS[c]
+            rest[c, f] = work.tile([P, 512 // w, w], F32, name="res", bufs=6, align_bytes=64)
+            if eng == "V":
+                nc.vector.tensor_copy(out=rest[c, f][:], in_=ob[c, f][:])
+            else:
+                nc.scalar.copy(out=rest[c, f][:], in_=ob[c, f][:])
+
+        def store(c, f):
+            lo, w = CHUNKS[c]
+            nt = 512 // w
+            nc.sync.dma_start(
+                out=out[f * P : (f + nt) * P, lo : lo + w].rearrange("(j p) n -> p j n", p=P), in_=rest[c, f][:]
+            )
+
+
+        load_es()
+        es_prep()
+        load_rg()
+        r_prep()
+        load_pb()
+        load_x(0, 0, 1)
+        r_diag(1)
+        pb_prep()
+        x_mul(0)
+        load_e(0)
+        e_mul(0)
+        load_x(0, 1, 2)
+        x_mul(1)
+        x_turn(0)
+        load_x(0, 2, 4)
+        x_turn(1)
+        r_mul_s(0, 0)
+        r_mul_s(0, 1)
+        e_turn(0, 1)
+        x_copy(0)
+        x_copy(1)
+        e_mul(3)
+        e_mul(2)
+        e_turn(2, 2)
+        e_copy(2, 2)
+        load_w(0, 512)
+        x_mul(2)
+        load_scales2()
+        x_turn(2)
+        x_mul(3)
+        e_mul(1)
+        load_x(1, 0, 2)
+        e_copy(0, 1)
+        x_mul(5)
+        load_e(1)
+        load_scales1()
+        x_mul(4)
+        x_turn(3)
+        x_copy(2)
+        x_quant1(0)
+        e_neg(0, 1)
+        e_quant(0, 1)
+        load_w(512, 1024)
+        x_quant1(1)
+        e_turn(1, 1)
+        e_copy(1, 1)
+        r_mul_s(0, 2)
+        e_neg(1, 1)
+        x_turn(5)
+        e_quant(1, 1)
+        x_copy(3)
+        e_mul(4)
+        x_turn(4)
+        x_copy(4)
+        x_copy(5)
+        s1(0, 0, 1)
+        s1(0, 0, 0)
+        tanh(0, 0, 1)
+        e_neg(2, 2)
+        s1(1, 0, 1)
+        tanh(1, 0, 1)
+        e_mul(5)
+        s1(1, 0, 0)
+        tanh(0, 0, 0)
+        tanh(1, 0, 0)
+        x_quant(1)
+        e_turn(4, 2)
+        r_mul_s(0, 3)
+        e_copy(4, 2)
+        load_x(1, 2, 4)
+        e_quant(2, 2)
+        s1(3, 0, 0)
+        e_mul(6)
+        tanh(3, 0, 0)
+        x_mul(6)
+        s1(2, 0, 1)
+        e_mul(7)
+        x_mul(7)
+        x_turn(6)
+        x_copy(6)
+        e_neg(4, 2)
+        x_quant(2)
+        e_turn(6, 2)
+        e_copy(6, 2)
+        x_turn(7)
+        x_copy(7)
+        r_pe(1, 1)
+        e_quant(4, 2)
+        s1(5, 0, 1)
+        x_quant(3)
+        tanh(2, 0, 1)
+        tanh(5, 0, 1)
+        e_neg(6, 2)
+        r_pe(1, 0)
+        e_quant(6, 2)
+        r_weave(0, 0)
+        r_weave(0, 3)
+        r_weave(0, 1)
+        r_copy(1, 0)
+        r_copy(1, 1)
+        s1(3, 0, 1)
+        r_weave(0, 2)
+        s1(5, 0, 0)
+        tanh(3, 0, 1)
+        tanh(5, 0, 0)
+        gs_prep()
+        diff(0, 0, 0, 2)
+        scale_v(0, 0, 0)
+        scale_v(0, 0, 1)
+        s1(4, 0, 0)
+        tanh(4, 0, 0)
+        s1(2, 0, 0)
+        tanh(2, 0, 0)
+        s1(2, 1, 0)
+        tanh(2, 1, 0)
+        s1(4, 0, 1)
+        s1(7, 0, 0)
+        s1(6, 0, 0)
+        tanh(4, 0, 1)
+        diff(0, 0, 2, 4)
+        diff(1, 0, 0, 2)
+        tanh(7, 0, 0)
+        scale_v(0, 0, 3)
+        r_quant(0, 0, 1024)
+        tanh(6, 0, 0)
+        s1(6, 0, 1)
+        tanh(6, 0, 1)
+        scale_v(0, 0, 2)
+        scale_s(1, 0, 0)
+        scale_s(1, 0, 1)
+        s1(7, 0, 1)
+        tanh(7, 0, 1)
+        diff(1, 0, 2, 4)
+        s1(3, 1, 0)
+        tanh(3, 1, 0)
+        weave_d(0, 0, 0, 256)
+        s1(0, 1, 0)
+        tanh(0, 1, 0)
+        s1(1, 1, 0)
+        s1(0, 1, 1)
+        tanh(1, 1, 0)
+        scale_s(1, 0, 2)
+        tanh(0, 1, 1)
+        s1(1, 1, 1)
+        weave_d(0, 0, 256, 512)
+        quant_d(0, 0)
+        tanh(1, 1, 1)
+        diff(0, 1, 0, 2)
+        s1(3, 1, 1)
+        s1(2, 1, 1)
+        scale_s(1, 0, 3)
+        weave_d(1, 0, 0, 256)
+        r_pe(1, 2)
+        weave_d(1, 0, 256, 512)
+        tanh(3, 1, 1)
+        tanh(2, 1, 1)
+        diff(0, 1, 2, 4)
+        r_pe(1, 3)
+        r_copy(1, 2)
+        r_copy(1, 3)
+        s1(5, 1, 1)
+        scale_v(0, 1, 0)
+        scale_v(0, 1, 1)
+        scale_v(0, 1, 3)
+        s1(6, 1, 0)
+        tanh(5, 1, 1)
+        s1(5, 1, 0)
+        tanh(5, 1, 0)
+        tanh(6, 1, 0)
+        quant_d(1, 0)
+        s1(4, 1, 0)
+        tanh(4, 1, 0)
+        scale_v(0, 1, 2)
+        s1(4, 1, 1)
+        tanh(4, 1, 1)
+        s1(7, 1, 0)
+        tanh(7, 1, 0)
+        s1(7, 1, 1)
+        tanh(7, 1, 1)
+        s2(0, 0, 0, "m")
+        r_quant(1, 0, 1024)
+        s2(0, 0, 1, "m")
+        out_copy(0, 0, "S")
+        s1(6, 1, 1)
+        store(0, 0)
+        weave_d(0, 1, 0, 256)
+        weave_d(0, 1, 256, 512)
+        s2(0, 5, 0, "m")
+        diff(1, 1, 0, 2)
+        tanh(6, 1, 1)
+        s2(0, 5, 1, "m")
+        out_copy(0, 5, "S")
+        store(0, 5)
+        s2(0, 7, 0, "m")
+        quant_d(0, 1)
+        s2(0, 7, 1, "m")
+        s2(0, 1, 0, "m")
+        out_copy(0, 7, "S")
+        store(0, 7)
+        scale_v(1, 1, 0)
+        scale_v(1, 1, 1)
+        s2(0, 1, 1, "m")
+        out_copy(0, 1, "S")
+        store(0, 1)
+        diff(1, 1, 2, 4)
+        scale_v(1, 1, 3)
+        s2(0, 6, 0, "m")
+        s2(0, 6, 1, "m")
+        out_copy(0, 6, "S")
+        scale_v(1, 1, 2)
+        s2(0, 2, 0, "m")
+        store(0, 6)
+        weave_d(1, 1, 0, 256)
+        quant_d(1, 1)
+        s2(0, 2, 1, "m")
+        s2(0, 4, 0, "m")
+        s2(0, 4, 1, "m")
+        out_copy(0, 2, "S")
+        store(0, 2)
+        s2(0, 3, 0, "m")
+        s2(0, 3, 1, "m")
+        s2(1, 2, 0, "m")
+        s2(1, 0, 0, "m")
+        out_copy(0, 4, "S")
+        store(0, 4)
+        s2(1, 2, 1, "m")
+        out_copy(0, 3, "S")
+        store(0, 3)
+        s2(1, 3, 0, "m")
+        s2(1, 3, 1, "m")
+        out_copy(1, 2, "S")
+        quant_d(0, 2)
+        s2(1, 0, 1, "m")
+        s2(1, 1, 0, "m")
+        s2(1, 1, 1, "m")
+        out_copy(1, 0, "S")
+        s2_last(2, 1, 0, "u")
+        store(1, 2)
+        weave_d(1, 1, 256, 512)
+        quant_d(1, 2)
+        s2(1, 4, 0, "m")
+        s2(1, 4, 1, "m")
+        s2(1, 5, 0, "m")
+        s2_last(2, 0, 0, "m")
+        s2_last(2, 0, 1, "m")
+        s2_last(2, 1, 1, "u")
+        s2(1, 5, 1, "m")
+        s2_last(2, 6, 0, "m")
+        s2_last(2, 4, 0, "m")
+        s2_last(2, 4, 1, "m")
+        s2_last(2, 7, 0, "u")
+        s2_last(2, 7, 1, "u")
+        s2_last(2, 6, 1, "m")
+        store(1, 0)
+        copy_last(2, 0, "S")
+        copy_last(2, 1, "V")
+        store(2, 0)
+        s2_last(2, 5, 0, "u")
+        out_copy(1, 4, "S")
+        s2_last(2, 5, 1, "u")
+        s2_last(2, 3, 0, "u")
+        s2_last(2, 3, 1, "u")
+        s2(1, 6, 0, "m")
+        s2(1, 6, 1, "m")
+        s2_last(2, 2, 0, "m")
+        s2_last(2, 2, 1, "m")
+        store(1, 4)
+        copy_last(2, 6, "S")
+        copy_last(2, 7, "V")
+        store(2, 6)
+        copy_last(2, 4, "S")
+        copy_last(2, 5, "V")
+        s2(1, 7, 0, "m")
+        s2(1, 7, 1, "m")
+        store(2, 4)
+        copy_last(2, 2, "S")
+        copy_last(2, 3, "V")
+        out_copy(1, 6, "S")
+        store(2, 2)
+        store(1, 6)

@@ -37,9 +37,11 @@ def tile_centredequilibriumpropupdate_w4_kernel(
 
         xt = [keep.tile([P, T, D], BF16, name="xt%d" % i, align_bytes=64) for i in range(G)]
         eb = keep.tile([P, G, T, O], U8, name="eb", align_bytes=64)
-        pb = keep.tile([P, D], BF16, name="pb", align_bytes=64)
+        prow = keep.tile([P, D], BF16, name="prow", align_bytes=64)
+        erow = keep.tile([P, O], F32, name="erow", align_bytes=64)
+        ones_bf = keep.tile([P, P], BF16, name="ones_bf", align_bytes=64)
+        ones_f = keep.tile([P, P], F32, name="ones_f", align_bytes=64)
         pbp = keep.tile([P, D], BF16, name="pbp", align_bytes=64)
-        es_raw = keep.tile([P, O], F32, name="es_raw", align_bytes=64)
         es_half = keep.tile([P, O], F32, name="es_half", align_bytes=64)
         w1t = keep.tile([P, 2, 2 * H], U8, name="w1t", align_bytes=64)
         w2t = keep.tile([P, 2 * H], U8, name="w2t", align_bytes=64)
@@ -75,20 +77,18 @@ def tile_centredequilibriumpropupdate_w4_kernel(
 
 
         ident_bf = keep.tile([P, P], BF16, name="ident_bf", align_bytes=64)
-        nc.gpsimd.memset(wsc[:].rearrange("p k n -> p (k n)").bitcast(I32), 0)
+        nc.vector.memset(prow[:].bitcast(I32), 0)
+        nc.gpsimd.memset(erow[:], 0.0)
+        nc.vector.memset(ones_bf[:], 1.0)
+        nc.vector.memset(warm[:], 0.0)
+        nc.vector.memset(wsc[:].rearrange("p k n -> p (k n)").bitcast(I32), 0)
+        nc.gpsimd.memset(ones_f[:], 1.0)
         make_identity(nc, ident[:])
         make_identity(nc, ident_bf[:])
-        nc.vector.memset(warm[:], 0.0)
         nc.scalar.activation(out=warm[:, 1:2], in_=warm[:, 0:1], func=TANH)
 
         def load_x(i, t0, t1):
             nc.sync.dma_start(out=xt[i][:, t0:t1, :], in_=xv[i, :, t0:t1, :])
-
-        def load_pb():
-            nc.sync.dma_start(out=pb[:], in_=p.partition_broadcast(P))
-
-        def load_es():
-            nc.sync.dma_start(out=es_raw[:], in_=e_scale.rearrange("o k -> (o k)").partition_broadcast(P))
 
         def load_e(i):
             nc.sync.dma_start(out=eb[:, i, :, :], in_=ev[i])
@@ -109,15 +109,55 @@ def tile_centredequilibriumpropupdate_w4_kernel(
                     out=wsc[32 * q : 32 * q + 4, 2, :].bitcast(I32), in_=w2_scales[0, 4 * q : 4 * q + 4, :].bitcast(I32)
                 )
 
+        def load_prow():
+            nc.sync.dma_start(out=prow[0:1, :], in_=p.rearrange("(o d) -> o d", o=1))
+
+        def load_erow():
+            nc.sync.dma_start(out=erow[0:1, :], in_=e_scale)
+
+        load_prow()
+        load_x(0, 0, 1)
+        load_erow()
+        load_e(0)
+        load_x(0, 1, 2)
+        load_w(0, W)
+        load_scales1()
+        load_scales2()
+        load_x(0, 2, 4)
+        load_rg()
+        load_e(1)
+        load_x(1, 0, 2)
+        load_x(1, 2, 4)
+        load_w(W, H)
         xpw = {}
+        pbk = {}
         eww = {}
         xg = {}
         eg = {}
         xb = {}
         ebk = {}
 
-        def es_prep():
-            nc.scalar.activation(out=es_half[:], in_=es_raw[:], func=COPY, scale=0.5)
+        def ones_p():
+            for j in range(2):
+                pbk[j] = psum.tile([P, 512], F32, name="m")
+                nc.tensor.matmul(
+                    pbk[j][:], lhsT=ones_bf[:], rhs=prow[:, 512 * j : 512 * (j + 1)], start=True, stop=True
+                )
+
+        def pb_copy(j, eng):
+            dst = pbp[:].rearrange("p (u q e) -> p u q e", u=2, e=2)[:, :, 128 * j : 128 * (j + 1), :]
+            src = pbk[j][:].rearrange("p (q u e) -> p u q e", u=2, e=2)
+            if eng == "V":
+                nc.vector.tensor_copy(out=dst, in_=src)
+            else:
+                nc.scalar.copy(out=dst, in_=src)
+
+        def ones_e():
+            pbk[2] = psum.tile([P, O], F32, name="m")
+            nc.tensor.matmul(pbk[2][:], lhsT=ones_f[:], rhs=erow[:], start=True, stop=True)
+
+        def es_copy():
+            nc.scalar.activation(out=es_half[:], in_=pbk[2][:], func=COPY, scale=0.5)
 
         def gs_prep():
             nc.scalar.activation(
@@ -125,12 +165,6 @@ def tile_centredequilibriumpropupdate_w4_kernel(
                 in_=gb[:].rearrange("p g t -> p (g t)"),
                 func=COPY,
                 scale=1.0 / 32.0,
-            )
-
-        def pb_prep():
-            nc.vector.tensor_copy(
-                out=pbp[:].rearrange("p (u q e) -> p u q e", u=2, e=2),
-                in_=pb[:].rearrange("p (q u e) -> p u q e", u=2, e=2),
             )
 
         def x_mul(b):
@@ -395,283 +429,271 @@ def tile_centredequilibriumpropupdate_w4_kernel(
             )
 
 
-        load_es()
-        es_prep()
-        load_rg()
-        r_prep()
-        load_pb()
-        load_x(0, 0, 1)
-        r_diag(1)
-        pb_prep()
-        x_mul(0)
-        load_e(0)
-        e_mul(0)
-        load_x(0, 1, 2)
+        ones_p()
+        pb_copy(0, "V")
+        pb_copy(1, "S")
         x_mul(1)
+        x_mul(0)
+        ones_e()
+        es_copy()
         x_turn(0)
-        load_x(0, 2, 4)
-        x_turn(1)
-        r_mul_s(0, 0)
-        r_mul_s(0, 1)
-        e_turn(0, 1)
         x_copy(0)
-        x_copy(1)
-        e_mul(3)
-        e_mul(2)
-        e_turn(2, 2)
-        e_copy(2, 2)
-        load_w(0, 512)
-        x_mul(2)
-        load_scales2()
-        x_turn(2)
-        x_mul(3)
-        e_mul(1)
-        load_x(1, 0, 2)
+        x_turn(1)
+        e_mul(0)
+        e_turn(0, 1)
         e_copy(0, 1)
-        x_mul(5)
-        load_e(1)
-        load_scales1()
-        x_mul(4)
-        x_turn(3)
-        x_copy(2)
-        x_quant1(0)
-        e_neg(0, 1)
-        e_quant(0, 1)
-        load_w(512, 1024)
-        x_quant1(1)
+        e_mul(1)
         e_turn(1, 1)
+        e_mul(3)
         e_copy(1, 1)
-        r_mul_s(0, 2)
+        e_mul(2)
+        x_quant1(0)
+        e_turn(2, 2)
         e_neg(1, 1)
-        x_turn(5)
-        e_quant(1, 1)
-        x_copy(3)
-        e_mul(4)
-        x_turn(4)
-        x_copy(4)
-        x_copy(5)
-        s1(0, 0, 1)
-        s1(0, 0, 0)
-        tanh(0, 0, 1)
-        e_neg(2, 2)
-        s1(1, 0, 1)
-        tanh(1, 0, 1)
-        e_mul(5)
-        s1(1, 0, 0)
-        tanh(0, 0, 0)
-        tanh(1, 0, 0)
-        x_quant(1)
-        e_turn(4, 2)
+        e_neg(0, 1)
+        x_mul(3)
+        x_copy(1)
+        x_mul(2)
+        x_turn(2)
+        e_copy(2, 2)
+        x_quant1(1)
+        r_prep()
+        r_mul_s(0, 0)
+        x_turn(3)
         r_mul_s(0, 3)
+        e_quant(0, 1)
+        e_mul(4)
+        e_mul(5)
+        r_mul_s(0, 2)
+        e_turn(4, 2)
         e_copy(4, 2)
-        load_x(1, 2, 4)
-        e_quant(2, 2)
-        s1(3, 0, 0)
-        e_mul(6)
-        tanh(3, 0, 0)
+        x_mul(4)
+        x_turn(4)
+        e_quant(1, 1)
+        s1(0, 0, 1)
+        e_neg(2, 2)
+        x_copy(4)
+        x_copy(2)
+        x_mul(5)
+        x_copy(3)
+        s1(0, 0, 0)
         x_mul(6)
-        s1(2, 0, 1)
+        r_mul_s(0, 1)
+        tanh(0, 0, 1)
+        s1(1, 0, 0)
         e_mul(7)
+        s1(1, 0, 1)
         x_mul(7)
-        x_turn(6)
-        x_copy(6)
-        e_neg(4, 2)
-        x_quant(2)
-        e_turn(6, 2)
-        e_copy(6, 2)
         x_turn(7)
-        x_copy(7)
-        r_pe(1, 1)
-        e_quant(4, 2)
-        s1(5, 0, 1)
-        x_quant(3)
-        tanh(2, 0, 1)
-        tanh(5, 0, 1)
-        e_neg(6, 2)
-        r_pe(1, 0)
-        e_quant(6, 2)
-        r_weave(0, 0)
-        r_weave(0, 3)
-        r_weave(0, 1)
-        r_copy(1, 0)
-        r_copy(1, 1)
-        s1(3, 0, 1)
-        r_weave(0, 2)
-        s1(5, 0, 0)
-        tanh(3, 0, 1)
-        tanh(5, 0, 0)
+        e_neg(4, 2)
         gs_prep()
-        diff(0, 0, 0, 2)
-        scale_v(0, 0, 0)
-        scale_v(0, 0, 1)
-        s1(4, 0, 0)
-        tanh(4, 0, 0)
+        e_mul(6)
+        e_turn(6, 2)
+        x_turn(5)
+        x_turn(6)
+        x_quant(1)
+        tanh(1, 0, 0)
+        e_quant(2, 2)
+        r_weave(0, 0)
+        r_weave(0, 2)
+        r_weave(0, 3)
+        tanh(0, 0, 0)
+        tanh(1, 0, 1)
+        x_copy(5)
+        x_quant(2)
+        e_copy(6, 2)
+        e_neg(6, 2)
         s1(2, 0, 0)
         tanh(2, 0, 0)
-        s1(2, 1, 0)
-        tanh(2, 1, 0)
+        s1(2, 0, 1)
+        x_copy(6)
+        x_copy(7)
+        tanh(2, 0, 1)
+        s1(3, 0, 1)
+        tanh(3, 0, 1)
+        r_weave(0, 1)
+        s1(3, 0, 0)
+        tanh(3, 0, 0)
+        e_quant(4, 2)
         s1(4, 0, 1)
-        s1(7, 0, 0)
-        s1(6, 0, 0)
+        diff(0, 0, 0, 2)
+        scale_s(0, 0, 0)
         tanh(4, 0, 1)
+        s1(5, 0, 0)
+        tanh(5, 0, 0)
+        s1(5, 0, 1)
+        s1(4, 0, 0)
+        tanh(5, 0, 1)
+        tanh(4, 0, 0)
+        x_quant(3)
         diff(0, 0, 2, 4)
-        diff(1, 0, 0, 2)
-        tanh(7, 0, 0)
-        scale_v(0, 0, 3)
-        r_quant(0, 0, 1024)
-        tanh(6, 0, 0)
+        scale_s(0, 0, 2)
+        e_quant(6, 2)
         s1(6, 0, 1)
         tanh(6, 0, 1)
-        scale_v(0, 0, 2)
-        scale_s(1, 0, 0)
-        scale_s(1, 0, 1)
+        r_mul(1, 0)
+        r_mul(1, 2)
+        s1(6, 0, 0)
+        tanh(6, 0, 0)
+        scale_s(0, 0, 1)
         s1(7, 0, 1)
         tanh(7, 0, 1)
-        diff(1, 0, 2, 4)
-        s1(3, 1, 0)
-        tanh(3, 1, 0)
-        weave_d(0, 0, 0, 256)
-        s1(0, 1, 0)
-        tanh(0, 1, 0)
-        s1(1, 1, 0)
-        s1(0, 1, 1)
-        tanh(1, 1, 0)
-        scale_s(1, 0, 2)
-        tanh(0, 1, 1)
-        s1(1, 1, 1)
-        weave_d(0, 0, 256, 512)
-        quant_d(0, 0)
-        tanh(1, 1, 1)
-        diff(0, 1, 0, 2)
-        s1(3, 1, 1)
-        s1(2, 1, 1)
-        scale_s(1, 0, 3)
-        weave_d(1, 0, 0, 256)
-        r_pe(1, 2)
-        weave_d(1, 0, 256, 512)
-        tanh(3, 1, 1)
-        tanh(2, 1, 1)
-        diff(0, 1, 2, 4)
-        r_pe(1, 3)
-        r_copy(1, 2)
-        r_copy(1, 3)
+        scale_s(0, 0, 3)
+        r_mul(1, 1)
         s1(5, 1, 1)
+        tanh(5, 1, 1)
+        r_mul(1, 3)
+        s1(7, 0, 0)
+        r_quant(0, 0, 1024)
+        s1(3, 1, 0)
+        r_weave(1, 0)
+        r_weave(1, 3)
+        diff(1, 0, 0, 2)
+        r_weave(1, 2)
+        s1(1, 1, 1)
+        tanh(7, 0, 0)
+        tanh(3, 1, 0)
+        r_weave(1, 1)
+        scale_s(1, 0, 0)
+        scale_s(1, 0, 1)
+        tanh(1, 1, 1)
+        weave_d(0, 0, 0, 256)
+        weave_d(0, 0, 256, 512)
+        s1(2, 1, 1)
+        tanh(2, 1, 1)
+        s1(0, 1, 0)
+        r_quant(1, 0, 1024)
+        diff(1, 0, 2, 4)
+        tanh(0, 1, 0)
+        s1(0, 1, 1)
+        tanh(0, 1, 1)
+        s1(1, 1, 0)
+        tanh(1, 1, 0)
+        s1(5, 1, 0)
+        quant_d(0, 0)
+        diff(0, 1, 0, 2)
+        scale_s(1, 0, 2)
+        scale_s(1, 0, 3)
+        tanh(5, 1, 0)
+        s1(4, 1, 0)
+        s1(3, 1, 1)
+        weave_d(1, 0, 0, 256)
+        weave_d(1, 0, 256, 512)
+        tanh(4, 1, 0)
         scale_v(0, 1, 0)
         scale_v(0, 1, 1)
-        scale_v(0, 1, 3)
-        s1(6, 1, 0)
-        tanh(5, 1, 1)
-        s1(5, 1, 0)
-        tanh(5, 1, 0)
-        tanh(6, 1, 0)
-        quant_d(1, 0)
-        s1(4, 1, 0)
-        tanh(4, 1, 0)
-        scale_v(0, 1, 2)
         s1(4, 1, 1)
         tanh(4, 1, 1)
-        s1(7, 1, 0)
-        tanh(7, 1, 0)
+        diff(1, 1, 0, 2)
+        tanh(3, 1, 1)
+        s1(2, 1, 0)
+        tanh(2, 1, 0)
+        s1(6, 1, 1)
+        tanh(6, 1, 1)
         s1(7, 1, 1)
         tanh(7, 1, 1)
-        s2(0, 0, 0, "m")
-        r_quant(1, 0, 1024)
-        s2(0, 0, 1, "m")
-        out_copy(0, 0, "S")
-        s1(6, 1, 1)
-        store(0, 0)
-        weave_d(0, 1, 0, 256)
-        weave_d(0, 1, 256, 512)
-        s2(0, 5, 0, "m")
-        diff(1, 1, 0, 2)
-        tanh(6, 1, 1)
-        s2(0, 5, 1, "m")
-        out_copy(0, 5, "S")
-        store(0, 5)
-        s2(0, 7, 0, "m")
-        quant_d(0, 1)
-        s2(0, 7, 1, "m")
-        s2(0, 1, 0, "m")
-        out_copy(0, 7, "S")
-        store(0, 7)
-        scale_v(1, 1, 0)
-        scale_v(1, 1, 1)
-        s2(0, 1, 1, "m")
-        out_copy(0, 1, "S")
-        store(0, 1)
-        diff(1, 1, 2, 4)
-        scale_v(1, 1, 3)
-        s2(0, 6, 0, "m")
-        s2(0, 6, 1, "m")
-        out_copy(0, 6, "S")
-        scale_v(1, 1, 2)
+        diff(0, 1, 2, 4)
+        s1(6, 1, 0)
+        tanh(6, 1, 0)
+        s1(7, 1, 0)
+        tanh(7, 1, 0)
+        quant_d(1, 0)
         s2(0, 2, 0, "m")
-        store(0, 6)
-        weave_d(1, 1, 0, 256)
-        quant_d(1, 1)
         s2(0, 2, 1, "m")
-        s2(0, 4, 0, "m")
-        s2(0, 4, 1, "m")
+        s2(0, 6, 0, "m")
+        scale_v(0, 1, 3)
         out_copy(0, 2, "S")
         store(0, 2)
+        scale_v(0, 1, 2)
+        scale_v(1, 1, 0)
+        scale_v(1, 1, 1)
+        s2(0, 6, 1, "m")
+        out_copy(0, 6, "S")
+        store(0, 6)
+        s2(0, 1, 0, "m")
+        s2(0, 1, 1, "m")
+        out_copy(0, 1, "S")
+        s2(0, 4, 0, "m")
+        s2(0, 4, 1, "m")
+        s2(0, 5, 0, "m")
+        s2(0, 5, 1, "m")
+        diff(1, 1, 2, 4)
+        s2(0, 7, 0, "m")
+        s2(0, 7, 1, "m")
         s2(0, 3, 0, "m")
+        store(0, 1)
         s2(0, 3, 1, "m")
-        s2(1, 2, 0, "m")
-        s2(1, 0, 0, "m")
+        weave_d(0, 1, 0, 256)
+        s2(0, 0, 0, "m")
+        s2(0, 0, 1, "m")
+        scale_v(1, 1, 2)
+        scale_v(1, 1, 3)
+        weave_d(1, 1, 0, 256)
         out_copy(0, 4, "S")
         store(0, 4)
-        s2(1, 2, 1, "m")
+        quant_d(0, 1)
+        s2(1, 2, 0, "m")
+        quant_d(1, 1)
+        out_copy(0, 5, "S")
+        store(0, 5)
+        out_copy(0, 7, "S")
+        store(0, 7)
         out_copy(0, 3, "S")
         store(0, 3)
-        s2(1, 3, 0, "m")
-        s2(1, 3, 1, "m")
-        out_copy(1, 2, "S")
-        quant_d(0, 2)
+        out_copy(0, 0, "S")
+        s2(1, 0, 0, "m")
         s2(1, 0, 1, "m")
         s2(1, 1, 0, "m")
         s2(1, 1, 1, "m")
+        s2(1, 2, 1, "m")
         out_copy(1, 0, "S")
-        s2_last(2, 1, 0, "u")
-        store(1, 2)
+        weave_d(0, 1, 256, 512)
         weave_d(1, 1, 256, 512)
-        quant_d(1, 2)
-        s2(1, 4, 0, "m")
-        s2(1, 4, 1, "m")
-        s2(1, 5, 0, "m")
-        s2_last(2, 0, 0, "m")
-        s2_last(2, 0, 1, "m")
-        s2_last(2, 1, 1, "u")
-        s2(1, 5, 1, "m")
-        s2_last(2, 6, 0, "m")
+        s2(1, 3, 0, "m")
+        s2(1, 3, 1, "m")
+        out_copy(1, 2, "S")
+        store(0, 0)
+        s2(1, 6, 0, "m")
+        s2(1, 6, 1, "m")
+        s2(1, 7, 0, "m")
+        s2(1, 7, 1, "m")
+        out_copy(1, 6, "S")
+        store(1, 0)
+        quant_d(0, 2)
         s2_last(2, 4, 0, "m")
+        s2_last(2, 1, 0, "u")
+        s2_last(2, 5, 0, "u")
+        quant_d(1, 2)
         s2_last(2, 4, 1, "m")
+        copy_last(2, 4, "S")
+        s2_last(2, 5, 1, "u")
+        copy_last(2, 5, "V")
+        s2_last(2, 0, 0, "m")
+        store(1, 2)
+        s2_last(2, 6, 0, "m")
+        store(1, 6)
+        s2_last(2, 0, 1, "m")
+        copy_last(2, 0, "S")
+        store(2, 4)
+        s2_last(2, 1, 1, "u")
+        copy_last(2, 1, "V")
+        store(2, 0)
         s2_last(2, 7, 0, "u")
         s2_last(2, 7, 1, "u")
         s2_last(2, 6, 1, "m")
-        store(1, 0)
-        copy_last(2, 0, "S")
-        copy_last(2, 1, "V")
-        store(2, 0)
-        s2_last(2, 5, 0, "u")
-        out_copy(1, 4, "S")
-        s2_last(2, 5, 1, "u")
-        s2_last(2, 3, 0, "u")
-        s2_last(2, 3, 1, "u")
-        s2(1, 6, 0, "m")
-        s2(1, 6, 1, "m")
-        s2_last(2, 2, 0, "m")
-        s2_last(2, 2, 1, "m")
-        store(1, 4)
         copy_last(2, 6, "S")
         copy_last(2, 7, "V")
         store(2, 6)
-        copy_last(2, 4, "S")
-        copy_last(2, 5, "V")
-        s2(1, 7, 0, "m")
-        s2(1, 7, 1, "m")
-        store(2, 4)
+        s2_last(2, 3, 0, "u")
+        s2_last(2, 3, 1, "u")
+        s2_last(2, 2, 0, "m")
+        s2(1, 4, 0, "m")
+        s2_last(2, 2, 1, "m")
         copy_last(2, 2, "S")
         copy_last(2, 3, "V")
-        out_copy(1, 6, "S")
         store(2, 2)
-        store(1, 6)
+        s2(1, 4, 1, "m")
+        s2(1, 5, 0, "m")
+        s2(1, 5, 1, "m")
+        out_copy(1, 4, "S")
+        store(1, 4)

from contextlib import ExitStack

import concourse.mybir as mybir
from concourse.masks import make_identity

F32 = mybir.dt.float32
BF16 = mybir.dt.bfloat16
U32 = mybir.dt.uint32
I32 = mybir.dt.int32
U8 = mybir.dt.uint8
E4M3 = mybir.dt.float8_e4m3fn
FP8X4 = mybir.dt.float8_e4m3fn_x4
FP4X4 = mybir.dt.float4_e2m1fn_x4
MULT = mybir.AluOpType.mult
SUB = mybir.AluOpType.subtract
TANH = mybir.ActivationFunctionType.Tanh
COPY = mybir.ActivationFunctionType.Copy

P = 128
N, D, H, O = 1024, 1024, 1024, 512
FLOPS = 2 * N * D * H + 2 * N * O * H + 2 * N * D * H
G = 2
T = 4
W = 512
CHUNKS = ((0, 512), (512, 256), (768, 256))


def tile_centredequilibriumpropupdate_w4_kernel(
    tc, x, p, w1_words, w1_scales, e_bytes, e_scale, w2_words, w2_scales, r, g, out
):
    nc = tc.nc
    with ExitStack() as ctx:
        keep = ctx.enter_context(tc.tile_pool(name="keep", bufs=1))
        work = ctx.enter_context(tc.tile_pool(name="work", bufs=3))
        psum = ctx.enter_context(tc.psum_pool(name="psum", bufs=4))
        ctx.enter_context(tc.manual_schedule())

        xt = [keep.tile([P, T, D], BF16, name="xt%d" % i, align_bytes=64) for i in range(G)]
        eb = keep.tile([P, G, T, O], U8, name="eb", align_bytes=64)
        prow = keep.tile([P, D], BF16, name="prow", align_bytes=64)
        erow = keep.tile([P, O], F32, name="erow", align_bytes=64)
        ones_bf = keep.tile([P, P], BF16, name="ones_bf", align_bytes=64)
        ones_f = keep.tile([P, P], F32, name="ones_f", align_bytes=64)
        pbp = keep.tile([P, D], BF16, name="pbp", align_bytes=64)
        es_half = keep.tile([P, O], F32, name="es_half", align_bytes=64)
        w1t = keep.tile([P, 2, 2 * H], U8, name="w1t", align_bytes=64)
        w2t = keep.tile([P, 2 * H], U8, name="w2t", align_bytes=64)
        wsc = keep.tile([P, 3, H], U8, name="wsc", align_bytes=64)
        rb = keep.tile([P, G, T], BF16, name="rb", align_bytes=64)
        gb = keep.tile([P, G, T], BF16, name="gb", align_bytes=64)
        rf = keep.tile([P, G, T], F32, name="rf", align_bytes=64)
        gs = keep.tile([P, G, T], F32, name="gs", align_bytes=64)
        ident = keep.tile([P, P], F32, name="ident", align_bytes=64)
        warm = keep.tile([P, 2], F32, name="warm", align_bytes=64)
        xc = keep.tile([P, 8, 2, P], U32, name="xc", align_bytes=64)
        xs = keep.tile([P, 8, 2, P], U8, name="xs", align_bytes=64)
        ec = keep.tile([P, 8, 2, P], U32, name="ec", align_bytes=64)
        es = keep.tile([P, 8, 2, P], U8, name="es", align_bytes=64)
        rc = keep.tile([P, G, D], U32, name="rc", align_bytes=64)
        rs = keep.tile([P, G, D], U8, name="rs", align_bytes=64)
        dc = [keep.tile([P, G, w], U32, name="dc%d" % c, align_bytes=64) for c, (lo, w) in enumerate(CHUNKS)]
        dsc = [keep.tile([P, G, w], U8, name="dsc%d" % c, align_bytes=64) for c, (lo, w) in enumerate(CHUNKS)]
        hpm = {
            (i, c, s): keep.tile([P, T, W], F32, name="h%d%d%d" % (i, c, s), align_bytes=64)
            for i in range(G)
            for c in range(2)
            for s in range(2)
        }

        xv = x.rearrange("(g p t) d -> g p t d", g=G, p=P, t=T)
        ev = e_bytes.rearrange("(g p t) o -> g p t o", g=G, p=P, t=T)
        w1v = w1_words.rearrange("g p w -> p g w")

        def load_w(lo, hi):
            nc.sync.dma_start(out=w1t[:, :, 2 * lo : 2 * hi], in_=w1v[:, :, 2 * lo : 2 * hi])
            nc.sync.dma_start(out=w2t[:, 2 * lo : 2 * hi], in_=w2_words[0, :, 2 * lo : 2 * hi])


        ident_bf = keep.tile([P, P], BF16, name="ident_bf", align_bytes=64)
        nc.vector.memset(prow[:].bitcast(I32), 0)
        nc.gpsimd.memset(erow[:], 0.0)
        nc.vector.memset(ones_bf[:], 1.0)
        nc.vector.memset(warm[:], 0.0)
        nc.vector.memset(wsc[:].rearrange("p k n -> p (k n)").bitcast(I32), 0)
        nc.gpsimd.memset(ones_f[:], 1.0)
        make_identity(nc, ident[:])
        make_identity(nc, ident_bf[:])
        nc.scalar.activation(out=warm[:, 1:2], in_=warm[:, 0:1], func=TANH)

        def load_x(i, t0, t1):
            nc.sync.dma_start(out=xt[i][:, t0:t1, :], in_=xv[i, :, t0:t1, :])

        def load_e(i):
            nc.sync.dma_start(out=eb[:, i, :, :], in_=ev[i])

        def load_rg():
            nc.sync.dma_start(out=rb[:], in_=r.rearrange("(g p t) -> p g t", g=G, p=P, t=T))
            nc.sync.dma_start(out=gb[:], in_=g.rearrange("(g p t) -> p g t", g=G, p=P, t=T))

        def load_scales1():
            for q in range(4):
                nc.sync.dma_start(
                    out=wsc[32 * q : 32 * q + 4, 0:2, :].bitcast(I32),
                    in_=w1_scales[:, 4 * q : 4 * q + 4, :].rearrange("g q n -> q g n").bitcast(I32),
                )
        def load_scales2():
            for q in range(4):
                nc.sync.dma_start(
                    out=wsc[32 * q : 32 * q + 4, 2, :].bitcast(I32), in_=w2_scales[0, 4 * q : 4 * q + 4, :].bitcast(I32)
                )

        def load_prow():
            nc.sync.dma_start(out=prow[0:1, :], in_=p.rearrange("(o d) -> o d", o=1))

        def load_erow():
            nc.sync.dma_start(out=erow[0:1, :], in_=e_scale)

        load_prow()
        load_x(0, 0, 1)
        load_erow()
        load_e(0)
        load_x(0, 1, 2)
        load_w(0, W)
        load_scales1()
        load_scales2()
        load_x(0, 2, 4)
        load_rg()
        load_e(1)
        load_x(1, 0, 2)
        load_x(1, 2, 4)
        load_w(W, H)
        xpw = {}
        pbk = {}
        eww = {}
        xg = {}
        eg = {}
        xb = {}
        ebk = {}

        def ones_p():
            for j in range(2):
                pbk[j] = psum.tile([P, 512], F32, name="m")
                nc.tensor.matmul(
                    pbk[j][:], lhsT=ones_bf[:], rhs=prow[:, 512 * j : 512 * (j + 1)], start=True, stop=True
                )

        def pb_copy(j, eng):
            dst = pbp[:].rearrange("p (u q e) -> p u q e", u=2, e=2)[:, :, 128 * j : 128 * (j + 1), :]
            src = pbk[j][:].rearrange("p (q u e) -> p u q e", u=2, e=2)
            if eng == "V":
                nc.vector.tensor_copy(out=dst, in_=src)
            else:
                nc.scalar.copy(out=dst, in_=src)

        def ones_e():
            pbk[2] = psum.tile([P, O], F32, name="m")
            nc.tensor.matmul(pbk[2][:], lhsT=ones_f[:], rhs=erow[:], start=True, stop=True)

        def es_copy():
            nc.scalar.activation(out=es_half[:], in_=pbk[2][:], func=COPY, scale=0.5)

        def gs_prep():
            nc.scalar.activation(
                out=gs[:].rearrange("p g t -> p (g t)"),
                in_=gb[:].rearrange("p g t -> p (g t)"),
                func=COPY,
                scale=1.0 / 32.0,
            )

        def x_mul(b):
            xp = work.tile([P, D], BF16, name="xp", align_bytes=64)
            nc.vector.tensor_tensor(
                out=xp[:].rearrange("p (u q e) -> p u q e", u=2, e=2),
                in0=xt[b // T][:, b % T, :].rearrange("p (q u e) -> p u q e", u=2, e=2),
                in1=pbp[:].rearrange("p (u q e) -> p u q e", u=2, e=2),
                op=MULT,
            )
            xpw[b] = xp

        def e_mul(b):
            ew = work.tile([P, O], BF16, name="ew", align_bytes=64)
            nc.vector.tensor_tensor(out=ew[:], in0=eb[:, b // T, b % T, :].bitcast(E4M3), in1=es_half[:], op=MULT)
            eww[b] = ew

        def x_turn(b):
            xb[b] = psum.tile([P, 2, 2, P], F32, name="m")
            words = xpw[b][:].bitcast(F32)
            for k in range(2):
                for u in range(2):
                    nc.tensor.transpose(xb[b][:, k, u, :], words[:, 256 * u + 128 * k : 256 * u + 128 * (k + 1)], ident[:])

        def x_copy(b):
            if b % 2 == 0:
                xg[b // 2] = work.tile([P, 2, 2, P, 4], BF16, name="xg", bufs=2, align_bytes=64)
            grouped = xg[b // 2][:, b % 2].rearrange("p k n j -> p k (n j)").bitcast(F32)
            nc.scalar.copy(
                out=grouped.rearrange("p k (n u) -> p k n u", u=2), in_=xb[b][:].rearrange("p k u n -> p k n u")
            )

        def e_turn(b, n):
            ebk[b] = psum.tile([P, n, 2, P], F32, name="m")
            for j in range(n):
                words = eww[b + j][:].bitcast(F32)
                for u in range(2):
                    nc.tensor.transpose(ebk[b][:, j, u, :], words[:, u:256:2], ident[:])

        def e_copy(b, n):
            if b % 2 == 0:
                eg[b // 2] = work.tile([P, 2, 2, P, 4], BF16, name="eg", bufs=2, align_bytes=64)
            h = b % 2
            grouped = eg[b // 2][:, h : h + n, 0].rearrange("p b n j -> p b (n j)").bitcast(F32)
            nc.scalar.copy(
                out=grouped.rearrange("p b (n u) -> p b n u", u=2), in_=ebk[b][:].rearrange("p b u n -> p b n u")
            )

        def x_quant(q):
            nc.vector.quantize_mx(
                out=xc[:, 2 * q : 2 * q + 2].rearrange("p b k n -> p (b k n)").bitcast(FP8X4),
                scales=xs[:, 2 * q : 2 * q + 2].rearrange("p b k n -> p (b k n)"),
                in_=xg[q][:].rearrange("p b k n j -> p (b k n j)"),
            )

        def x_quant1(b):
            nc.vector.quantize_mx(
                out=xc[:, b].rearrange("p k n -> p (k n)").bitcast(FP8X4),
                scales=xs[:, b].rearrange("p k n -> p (k n)"),
                in_=xg[b // 2][:, b % 2].rearrange("p k n j -> p (k n j)"),
            )

        def e_neg(b, n):
            h = b % 2
            flat = eg[b // 2][:, h : h + n].rearrange("p b s n j -> p b s (n j)")
            nc.vector.tensor_scalar(out=flat[:, :, 1], in0=flat[:, :, 0], scalar1=-1.0, scalar2=None, op0=MULT)

        def e_quant(b, n):
            h = b % 2
            nc.vector.quantize_mx(
                out=ec[:, b : b + n].rearrange("p b s n -> p (b s n)").bitcast(FP8X4),
                scales=es[:, b : b + n].rearrange("p b s n -> p (b s n)"),
                in_=eg[b // 2][:, h : h + n].rearrange("p b s n j -> p (b s n j)"),
            )

        ub = {}

        def s1(b, c, s):
            lo, hi = c * W, (c + 1) * W
            ub[b, c, s] = psum.tile([P, W], F32, name="u")
            for k in range(2):
                nc.tensor.matmul_mx(
                    out=ub[b, c, s][:],
                    lhsT=xc[:, b, k, :].bitcast(FP8X4),
                    lhsT_scale=xs[:, b, k, :],
                    rhs=w1t[:, k, 2 * lo : 2 * hi].bitcast(FP4X4),
                    rhs_scale=wsc[:, k, lo:hi],
                    start=(k == 0),
                    stop=False,
                )
            nc.tensor.matmul_mx(
                out=ub[b, c, s][:],
                lhsT=ec[:, b, s, :].bitcast(FP8X4),
                lhsT_scale=es[:, b, s, :],
                rhs=w2t[:, 2 * lo : 2 * hi].bitcast(FP4X4),
                rhs_scale=wsc[:, 2, lo:hi],
                start=False,
                stop=True,
            )

        def tanh(b, c, s):
            nc.scalar.activation(out=hpm[b // T, c, s][:, b % T, :], in_=ub[b, c, s][:], func=TANH)

        db = {}
        dg = {}

        def diff(i, c, t0, t1):
            nc.vector.tensor_tensor(
                out=hpm[i, c, 0][:, t0:t1, :], in0=hpm[i, c, 0][:, t0:t1, :], in1=hpm[i, c, 1][:, t0:t1, :], op=SUB
            )

        def new_db(i, c):
            if (i, c) not in db:
                db[i, c] = work.tile([P, T, W], BF16, name="db", bufs=3, align_bytes=64)

        def scale_s(i, c, t):
            new_db(i, c)
            nc.scalar.activation(out=db[i, c][:, t, :], in_=hpm[i, c, 0][:, t, :], func=COPY, scale=gs[:, i, t : t + 1])

        def scale_v(i, c, t):
            new_db(i, c)
            nc.vector.tensor_scalar(
                out=db[i, c][:, t, :], in0=hpm[i, c, 0][:, t, :], scalar1=gs[:, i, t : t + 1], scalar2=None, op0=MULT
            )

        def weave_d(i, c, lo, hi):
            if lo == 0:
                dg[i, c] = work.tile([P, W, T], BF16, name="dg", bufs=3, align_bytes=64)
            nc.vector.tensor_copy(
                out=dg[i, c][:, lo:hi, :].rearrange("p (n j) t -> p n t j", j=4),
                in_=db[i, c][:, :, lo:hi].rearrange("p t (n j) -> p n t j", j=4),
            )

        def quant_d(i, c):
            lo, w = CHUNKS[c]
            nc.vector.quantize_mx(
                out=dc[c][:, i, :].bitcast(FP8X4),
                scales=dsc[c][:, i, :],
                in_=dg[i, lo // W][:, lo % W : lo % W + w, :].rearrange("p n t -> p (n t)"),
            )

        xm = {}
        xw = {}
        rdiag = {}
        rbk = {}

        def new_xw(i):
            if i not in xw:
                xw[i] = work.tile([P, D, T], BF16, name="xw", bufs=2, align_bytes=64)

        def r_mul(i, t):
            if i not in xm:
                xm[i] = work.tile([P, T, D], BF16, name="xm", bufs=1, align_bytes=64)
            nc.vector.tensor_scalar(
                out=xm[i][:, t, :], in0=xt[i][:, t, :], scalar1=rb[:, i, t : t + 1], scalar2=None, op0=MULT
            )

        def r_prep():
            nc.scalar.activation(
                out=rf[:].rearrange("p g t -> p (g t)"), in_=rb[:].rearrange("p g t -> p (g t)"), func=COPY
            )

        def r_mul_s(i, t):
            if i not in xm:
                xm[i] = work.tile([P, T, D], BF16, name="xm", bufs=1, align_bytes=64)
            nc.scalar.activation(out=xm[i][:, t, :], in_=xt[i][:, t, :], func=COPY, scale=rf[:, i, t : t + 1])

        def r_weave(i, q):
            new_xw(i)
            w = D // 4
            nc.vector.tensor_copy(
                out=xw[i][:, q * w : (q + 1) * w, :].rearrange("p (n j) t -> p n t j", j=4),
                in_=xm[i][:, :, q * w : (q + 1) * w].rearrange("p t (n j) -> p n t j", j=4),
            )

        def r_diag(i):
            rdiag[i] = work.tile([P, T, P], BF16, name="rdiag", bufs=2, align_bytes=64)
            for t in range(T):
                nc.vector.tensor_scalar(
                    out=rdiag[i][:, t, :], in0=ident_bf[:], scalar1=rb[:, i, t : t + 1], scalar2=None, op0=MULT
                )

        def r_pe(i, q):
            w = D // 4
            rbk[i, q] = psum.tile([P, T, w], BF16, name="m")
            for t in range(T):
                nc.tensor.matmul(
                    rbk[i, q][:, t, :],
                    lhsT=rdiag[i][:, t, :],
                    rhs=xt[i][:, t, q * w : (q + 1) * w],
                    start=True,
                    stop=True,
                )

        def r_copy(i, q):
            new_xw(i)
            w = D // 4
            nc.scalar.copy(
                out=xw[i][:, q * w : (q + 1) * w, :], in_=rbk[i, q][:].rearrange("p t n -> p n t")
            )

        def r_quant(i, lo, hi):
            nc.vector.quantize_mx(
                out=rc[:, i, lo:hi].bitcast(FP8X4), scales=rs[:, i, lo:hi], in_=xw[i][:, lo:hi, :].rearrange("p n t -> p (n t)")
            )

        ob = {}
        rest = {}

        def s2_last(c, f, i, tag):
            lo, w = CHUNKS[c]
            if i == 0:
                ob[c, f] = psum.tile([P, w], F32, name=tag)
            nc.tensor.matmul_mx(
                out=ob[c, f][:],
                lhsT=rc[:, i, f * P : (f + 1) * P].bitcast(FP8X4),
                lhsT_scale=rs[:, i, f * P : (f + 1) * P],
                rhs=dc[c][:, i, :].bitcast(FP8X4),
                rhs_scale=dsc[c][:, i, :],
                start=(i == 0),
                stop=(i == G - 1),
            )

        def copy_last(c, f, eng):
            lo, w = CHUNKS[c]
            if f % 2 == 0:
                rest[c, f] = work.tile([P, 2, w], F32, name="resl", bufs=4, align_bytes=64)
            dst = rest[c, f - f % 2][:, f % 2, :]
            if eng == "V":
                nc.vector.tensor_copy(out=dst, in_=ob[c, f][:])
            else:
                nc.scalar.copy(out=dst, in_=ob[c, f][:])

        def s2(c, f, i, tag):
            lo, w = CHUNKS[c]
            nt = 512 // w
            if i == 0 and f % nt == 0:
                ob[c, f] = psum.tile([P, nt, w], F32, name=tag)
            nc.tensor.matmul_mx(
                out=ob[c, f - f % nt][:, f % nt, :],
                lhsT=rc[:, i, f * P : (f + 1) * P].bitcast(FP8X4),
                lhsT_scale=rs[:, i, f * P : (f + 1) * P],
                rhs=dc[c][:, i, :].bitcast(FP8X4),
                rhs_scale=dsc[c][:, i, :],
                start=(i == 0),
                stop=(i == G - 1),
            )

        def out_copy(c, f, eng):
            lo, w = CHUNKS[c]
            rest[c, f] = work.tile([P, 512 // w, w], F32, name="res", bufs=6, align_bytes=64)
            if eng == "V":
                nc.vector.tensor_copy(out=rest[c, f][:], in_=ob[c, f][:])
            else:
                nc.scalar.copy(out=rest[c, f][:], in_=ob[c, f][:])

        def store(c, f):
            lo, w = CHUNKS[c]
            nt = 512 // w
            nc.sync.dma_start(
                out=out[f * P : (f + nt) * P, lo : lo + w].rearrange("(j p) n -> p j n", p=P), in_=rest[c, f][:]
            )


        ones_p()
        pb_copy(0, "V")
        pb_copy(1, "S")
        x_mul(1)
        x_mul(0)
        ones_e()
        es_copy()
        x_turn(0)
        x_copy(0)
        x_turn(1)
        e_mul(0)
        e_turn(0, 1)
        e_copy(0, 1)
        e_mul(1)
        e_turn(1, 1)
        e_mul(3)
        e_copy(1, 1)
        e_mul(2)
        x_quant1(0)
        e_turn(2, 2)
        e_neg(1, 1)
        e_neg(0, 1)
        x_mul(3)
        x_copy(1)
        x_mul(2)
        x_turn(2)
        e_copy(2, 2)
        x_quant1(1)
        r_prep()
        r_mul_s(0, 0)
        x_turn(3)
        r_mul_s(0, 3)
        e_quant(0, 1)
        e_mul(4)
        e_mul(5)
        r_mul_s(0, 2)
        e_turn(4, 2)
        e_copy(4, 2)
        x_mul(4)
        x_turn(4)
        e_quant(1, 1)
        s1(0, 0, 1)
        e_neg(2, 2)
        x_copy(4)
        x_copy(2)
        x_mul(5)
        x_copy(3)
        s1(0, 0, 0)
        x_mul(6)
        r_mul_s(0, 1)
        tanh(0, 0, 1)
        s1(1, 0, 0)
        e_mul(7)
        s1(1, 0, 1)
        x_mul(7)
        x_turn(7)
        e_neg(4, 2)
        gs_prep()
        e_mul(6)
        e_turn(6, 2)
        x_turn(5)
        x_turn(6)
        x_quant(1)
        tanh(1, 0, 0)
        e_quant(2, 2)
        r_weave(0, 0)
        r_weave(0, 2)
        r_weave(0, 3)
        tanh(0, 0, 0)
        tanh(1, 0, 1)
        x_copy(5)
        x_quant(2)
        e_copy(6, 2)
        e_neg(6, 2)
        s1(2, 0, 0)
        tanh(2, 0, 0)
        s1(2, 0, 1)
        x_copy(6)
        x_copy(7)
        tanh(2, 0, 1)
        s1(3, 0, 1)
        tanh(3, 0, 1)
        r_weave(0, 1)
        s1(3, 0, 0)
        tanh(3, 0, 0)
        e_quant(4, 2)
        s1(4, 0, 1)
        diff(0, 0, 0, 2)
        scale_s(0, 0, 0)
        tanh(4, 0, 1)
        s1(5, 0, 0)
        tanh(5, 0, 0)
        s1(5, 0, 1)
        s1(4, 0, 0)
        tanh(5, 0, 1)
        tanh(4, 0, 0)
        x_quant(3)
        diff(0, 0, 2, 4)
        scale_s(0, 0, 2)
        e_quant(6, 2)
        s1(6, 0, 1)
        tanh(6, 0, 1)
        r_mul(1, 0)
        r_mul(1, 2)
        s1(6, 0, 0)
        tanh(6, 0, 0)
        scale_s(0, 0, 1)
        s1(7, 0, 1)
        tanh(7, 0, 1)
        scale_s(0, 0, 3)
        r_mul(1, 1)
        s1(5, 1, 1)
        tanh(5, 1, 1)
        r_mul(1, 3)
        s1(7, 0, 0)
        r_quant(0, 0, 1024)
        s1(3, 1, 0)
        r_weave(1, 0)
        r_weave(1, 3)
        diff(1, 0, 0, 2)
        r_weave(1, 2)
        s1(1, 1, 1)
        tanh(7, 0, 0)
        tanh(3, 1, 0)
        r_weave(1, 1)
        scale_s(1, 0, 0)
        scale_s(1, 0, 1)
        tanh(1, 1, 1)
        weave_d(0, 0, 0, 256)
        weave_d(0, 0, 256, 512)
        s1(2, 1, 1)
        tanh(2, 1, 1)
        s1(0, 1, 0)
        r_quant(1, 0, 1024)
        diff(1, 0, 2, 4)
        tanh(0, 1, 0)
        s1(0, 1, 1)
        tanh(0, 1, 1)
        s1(1, 1, 0)
        tanh(1, 1, 0)
        s1(5, 1, 0)
        quant_d(0, 0)
        diff(0, 1, 0, 2)
        scale_s(1, 0, 2)
        scale_s(1, 0, 3)
        tanh(5, 1, 0)
        s1(4, 1, 0)
        s1(3, 1, 1)
        weave_d(1, 0, 0, 256)
        weave_d(1, 0, 256, 512)
        tanh(4, 1, 0)
        scale_v(0, 1, 0)
        scale_v(0, 1, 1)
        s1(4, 1, 1)
        tanh(4, 1, 1)
        diff(1, 1, 0, 2)
        tanh(3, 1, 1)
        s1(2, 1, 0)
        tanh(2, 1, 0)
        s1(6, 1, 1)
        tanh(6, 1, 1)
        s1(7, 1, 1)
        tanh(7, 1, 1)
        diff(0, 1, 2, 4)
        s1(6, 1, 0)
        tanh(6, 1, 0)
        s1(7, 1, 0)
        tanh(7, 1, 0)
        quant_d(1, 0)
        s2(0, 2, 0, "m")
        s2(0, 2, 1, "m")
        s2(0, 6, 0, "m")
        scale_v(0, 1, 3)
        out_copy(0, 2, "S")
        store(0, 2)
        scale_v(0, 1, 2)
        scale_v(1, 1, 0)
        scale_v(1, 1, 1)
        s2(0, 6, 1, "m")
        out_copy(0, 6, "S")
        store(0, 6)
        s2(0, 1, 0, "m")
        s2(0, 1, 1, "m")
        out_copy(0, 1, "S")
        s2(0, 4, 0, "m")
        s2(0, 4, 1, "m")
        s2(0, 5, 0, "m")
        s2(0, 5, 1, "m")
        diff(1, 1, 2, 4)
        s2(0, 7, 0, "m")
        s2(0, 7, 1, "m")
        s2(0, 3, 0, "m")
        store(0, 1)
        s2(0, 3, 1, "m")
        weave_d(0, 1, 0, 256)
        s2(0, 0, 0, "m")
        s2(0, 0, 1, "m")
        scale_v(1, 1, 2)
        scale_v(1, 1, 3)
        weave_d(1, 1, 0, 256)
        out_copy(0, 4, "S")
        store(0, 4)
        quant_d(0, 1)
        s2(1, 2, 0, "m")
        quant_d(1, 1)
        out_copy(0, 5, "S")
        store(0, 5)
        out_copy(0, 7, "S")
        store(0, 7)
        out_copy(0, 3, "S")
        store(0, 3)
        out_copy(0, 0, "S")
        s2(1, 0, 0, "m")
        s2(1, 0, 1, "m")
        s2(1, 1, 0, "m")
        s2(1, 1, 1, "m")
        s2(1, 2, 1, "m")
        out_copy(1, 0, "S")
        weave_d(0, 1, 256, 512)
        weave_d(1, 1, 256, 512)
        s2(1, 3, 0, "m")
        s2(1, 3, 1, "m")
        out_copy(1, 2, "S")
        store(0, 0)
        s2(1, 6, 0, "m")
        s2(1, 6, 1, "m")
        s2(1, 7, 0, "m")
        s2(1, 7, 1, "m")
        out_copy(1, 6, "S")
        store(1, 0)
        quant_d(0, 2)
        s2_last(2, 4, 0, "m")
        s2_last(2, 1, 0, "u")
        s2_last(2, 5, 0, "u")
        quant_d(1, 2)
        s2_last(2, 4, 1, "m")
        copy_last(2, 4, "S")
        s2_last(2, 5, 1, "u")
        copy_last(2, 5, "V")
        s2_last(2, 0, 0, "m")
        store(1, 2)
        s2_last(2, 6, 0, "m")
        store(1, 6)
        s2_last(2, 0, 1, "m")
        copy_last(2, 0, "S")
        store(2, 4)
        s2_last(2, 1, 1, "u")
        copy_last(2, 1, "V")
        store(2, 0)
        s2_last(2, 7, 0, "u")
        s2_last(2, 7, 1, "u")
        s2_last(2, 6, 1, "m")
        copy_last(2, 6, "S")
        copy_last(2, 7, "V")
        store(2, 6)
        s2_last(2, 3, 0, "u")
        s2_last(2, 3, 1, "u")
        s2_last(2, 2, 0, "m")
        s2(1, 4, 0, "m")
        s2_last(2, 2, 1, "m")
        copy_last(2, 2, "S")
        copy_last(2, 3, "V")
        store(2, 2)
        s2(1, 4, 1, "m")
        s2(1, 5, 0, "m")
        s2(1, 5, 1, "m")
        out_copy(1, 4, "S")
        store(1, 4)
